import numpy as np
import ml_dtypes


def mxq(x, axis, fmt="e4m3"):
    dtype, down = {"e4m3": (ml_dtypes.float8_e4m3fn, 7), "e5m2": (ml_dtypes.float8_e5m2, 14)}[fmt]
    v = np.moveaxis(np.asarray(x, np.float32).astype(ml_dtypes.bfloat16).astype(np.float64), axis, -1)
    blocks = v.reshape(v.shape[:-1] + (-1, 32))
    amax = np.abs(blocks).max(-1, keepdims=True)
    byte = np.maximum(np.where(amax > 0, np.frexp(amax)[1] - 1 + 127, 0) - down, 1)
    scale = np.exp2(byte - 127.0)
    codes = (blocks / scale).astype(np.float32).astype(dtype).astype(np.float64)
    return np.moveaxis((codes * scale).reshape(v.shape), -1, axis)


WIDE = False


def mx_kscale(k):
    if not WIDE:
        return np.ones(k)
    levels = np.array([10, -10, 5, -5, 0])
    if k % 512:
        return np.exp2(np.random.permutation(np.resize(levels, k // 32))).repeat(32)
    a = np.empty((k // 512, 16))
    for p in range(k // 512):
        a[p, :8] = np.random.permutation(np.resize(levels, 8))
        for g in range(8):
            far = levels[np.abs(levels - a[p, g]) >= 10]
            a[p, g + 8] = far[np.random.randint(len(far))]
    return np.exp2(a.ravel()).repeat(32)


def f64(x):
    return np.asarray(x).astype(np.float64)


def striped(idx):
    return np.tile(idx.reshape(-1, 16).T, (8, 1)).astype(np.uint16)


def unstriped(offs):
    return offs[:16].T.reshape(-1).astype(np.int64)


def relu(v):
    return np.maximum(v, 0.0)

def planes(y):
    n, m = y.shape
    v = y.astype(np.float32).astype(ml_dtypes.bfloat16).astype(np.float64).reshape(n // 32, 32, m)
    top = np.abs(v).max(1)
    byte = np.clip(np.where(top > 0, np.frexp(top)[1] - 1 + 127 - 7, 1), 1, 254)
    codes = (v * np.exp2(127.0 - byte)[:, None, :]).reshape(n, m).astype(np.float32).astype(ml_dtypes.float8_e4m3fn).view(np.uint8)
    words = codes.reshape(n // 512, 128, 4, m).transpose(0, 1, 3, 2)
    return np.ascontiguousarray(words), np.ascontiguousarray(byte.astype(np.uint8).reshape(n // 512, 16, m))


K, T, S, V, N = 512, 2048, 768, 256, 512
P = 2 ** 7


def setup_inputs():
    n = np.random.standard_normal
    s = mx_kscale(K)[:, None]
    return {
        "xT": (n((K, T)) * s).astype(np.float32),
        "w1": (n((K, N)) / np.sqrt(K) / s).astype(np.float32),
        "margin": np.tile(np.random.uniform(0.2, 2.0, V), (P, 1)).astype(np.float32),
        "offs": striped(np.random.permutation(T)[:S]),
    }


def reference(xT, w1, margin, offs):
    xq = mxq(f64(xT)[:, unstriped(offs)], 0, "e4m3")
    h = mxq(f64(w1), 0, "e4m3").T @ xq
    near = (h[:, :V] - h[:, V:2 * V]) ** 2
    far = (h[:, :V] - h[:, 2 * V:3 * V]) ** 2
    out_0 = relu(near - far + f64(margin)[:1])
    return (out_0,) + planes(out_0)

@@ -1,0 +1,147 @@
+from contextlib import ExitStack
+
+import concourse.mybir as mybir
+
+F32 = mybir.dt.float32
+BF16 = mybir.dt.bfloat16
+I32 = mybir.dt.int32
+U32 = mybir.dt.uint32
+U16 = mybir.dt.uint16
+U8 = mybir.dt.uint8
+FP8X4 = mybir.dt.float8_e4m3fn_x4
+ALU = mybir.AluOpType
+ACT = mybir.ActivationFunctionType
+
+P = 128
+K, T, V, N = 512, 2048, 256, 512
+H = V // 2
+FLOPS = 2 * K * N * 3 * V
+
+
+def tile_picked_triplet_none_lo_kernel(tc, xT, w1, margin, offs, out_0, out_1, out_2):
+    nc = tc.nc
+    with ExitStack() as ctx:
+        sb = ctx.enter_context(tc.tile_pool(name="sb", bufs=1))
+        ps = ctx.enter_context(tc.psum_pool(name="ps", bufs=1))
+
+        offsets = sb.tile([P, 3 * V // 16], U16, name="offsets")
+        x = [sb.tile([P, T], F32, name="x%d" % j) for j in range(4)]
+        w_raw = sb.tile([P, 4, N], F32, name="w_raw")
+        mg = sb.tile([P, V], F32, name="mg")
+        xv = xT.rearrange("(p j) t -> p j t", j=4)
+        nc.sync.dma_start(x[0][:], xv[:, 0, :])
+        nc.sync.dma_start(offsets[:], offs)
+        nc.sync.dma_start(x[1][:], xv[:, 1, :])
+        nc.sync.dma_start(w_raw[:], w1.rearrange("(p j) c -> p j c", j=4))
+        nc.sync.dma_start(x[2][:], xv[:, 2, :])
+        nc.sync.dma_start(x[3][:], xv[:, 3, :])
+        nc.sync.dma_start(mg[:], margin)
+
+        xb = [sb.tile([P, V, 4], BF16, name="xb%d" % r, align_bytes=64) for r in range(3)]
+        a_neg = sb.tile([P, H, 4], BF16, name="a_neg", align_bytes=64)
+        xc = [sb.tile([P, V], U32, name="xc%d" % r, align_bytes=64) for r in range(3)]
+        xs = [sb.tile([P, V], U8, name="xs%d" % r, align_bytes=64) for r in range(3)]
+        nc_codes = sb.tile([P, H], U32, name="nc_codes", align_bytes=64)
+        nc_scales = sb.tile([P, H], U8, name="nc_scales", align_bytes=64)
+        wb = [sb.tile([P, 2, P, 4], BF16, name="wb%d" % u, align_bytes=64) for u in range(2)]
+        wc = [sb.tile([P, 2 * P], U32, name="wc%d" % u, align_bytes=64) for u in range(2)]
+        ws = [sb.tile([P, 2 * P], U8, name="ws%d" % u, align_bytes=64) for u in range(2)]
+
+        def gather(j, r):
+            nc.vector.tensor_copy(xb[r][:, :, j], x[j][:].indirect(offsets[:, 16 * r : 16 * (r + 1)]))
+
+        def quantize(codes, scales, src):
+            nc.vector.quantize_mx(out=codes.bitcast(FP8X4), scales=scales, in_=src)
+
+        for j in range(2):
+            for r in range(3):
+                gather(j, r)
+
+        w_view = w_raw[:].rearrange("p j (m t) -> p m j t", t=4)
+        nc.vector.tensor_copy(wb[0][:].rearrange("p t m j -> p m j t"), w_view[:, :, :, 0:2])
+        nc.scalar.copy(wb[1][:].rearrange("p t m j -> p m j t"), w_view[:, :, :, 2:4])
+        for u in range(2):
+            quantize(wc[u][:], ws[u][:], wb[u][:].rearrange("p t m j -> p (t m j)"))
+
+        for r in range(3):
+            gather(2, r)
+
+        def passes(bank, terms):
+            for t in range(4):
+                cols = slice(P * (t % 2), P * (t % 2 + 1))
+                for i, (codes, scales) in enumerate(terms):
+                    nc.tensor.matmul_mx(
+                        out=bank[:, t, :],
+                        lhsT=wc[t // 2][:, cols].bitcast(FP8X4),
+                        lhsT_scale=ws[t // 2][:, cols],
+                        rhs=codes.bitcast(FP8X4),
+                        rhs_scale=scales,
+                        start=(i == 0),
+                        stop=(i == len(terms) - 1),
+                    )
+
+        lo, hi = slice(0, H), slice(H, V)
+        bank_a = ps.tile([P, 4, H], F32, name="bank_a")
+        bank_p = ps.tile([P, 4, H], F32, name="bank_p")
+        bank_n = ps.tile([P, 4, H], F32, name="bank_n")
+        bank_d1 = ps.tile([P, 4, H], F32, name="bank_d1")
+        bank_d2 = ps.tile([P, 4, H], F32, name="bank_d2")
+
+        def f32(name):
+            return sb.tile([P, 4, H], F32, name=name)
+
+        a_hi, d1_hi, d2_hi = f32("a_hi"), f32("d1_hi"), f32("d2_hi")
+        near = [f32("near0"), f32("near1")]
+        far = [f32("far0"), f32("far1")]
+        near_m = [f32("near_m0"), f32("near_m1")]
+        s = [f32("s0"), f32("s1")]
+        y = [f32("y0"), f32("y1")]
+        yb = [sb.tile([P, H, 4], BF16, name="yb%d" % h, align_bytes=64) for h in range(2)]
+        yc = [sb.tile([P, H], U32, name="yc%d" % h, align_bytes=64) for h in range(2)]
+        ys = sb.tile([P, V], U8, name="ys", align_bytes=64)
+
+        neg = (nc_codes[:], nc_scales[:])
+
+        gather(3, 0)
+        nc.scalar.activation(a_neg[:], xb[0][:, lo, :], ACT.Copy, scale=-1.0)
+        gather(3, 1)
+        quantize(xc[0][:, hi], xs[0][:, hi], xb[0][:, hi, :].rearrange("p v j -> p (v j)"))
+        quantize(xc[1][:], xs[1][:], xb[1][:].rearrange("p v j -> p (v j)"))
+        quantize(neg[0], neg[1], a_neg[:].rearrange("p v j -> p (v j)"))
+        passes(bank_a, [(xc[0][:, hi], xs[0][:, hi])])
+        passes(bank_p, [(xc[1][:, hi], xs[1][:, hi])])
+        passes(bank_d1, [neg, (xc[1][:, lo], xs[1][:, lo])])
+        gather(3, 2)
+        quantize(xc[2][:], xs[2][:], xb[2][:].rearrange("p v j -> p (v j)"))
+        passes(bank_n, [(xc[2][:, hi], xs[2][:, hi])])
+        passes(bank_d2, [neg, (xc[2][:, lo], xs[2][:, lo])])
+
+        def add_margin(h):
+            m = mg[:, H * h : H * (h + 1)].unsqueeze(1).to_broadcast([P, 4, H])
+            nc.vector.tensor_tensor(near_m[h][:], near[h][:], m, ALU.add)
+
+        nc.scalar.copy(a_hi[:], bank_a[:])
+        nc.scalar.activation(near[0][:], bank_d1[:], ACT.Square)
+        nc.vector.tensor_tensor(d1_hi[:], bank_p[:], a_hi[:], ALU.subtract)
+        nc.scalar.activation(near[1][:], d1_hi[:], ACT.Square)
+        add_margin(0)
+        nc.vector.tensor_tensor(d2_hi[:], bank_n[:], a_hi[:], ALU.subtract)
+        nc.scalar.activation(far[0][:], bank_d2[:], ACT.Square)
+        add_margin(1)
+        nc.scalar.activation(far[1][:], d2_hi[:], ACT.Square)
+
+        out_rows = out_0.rearrange("(p t) v -> p t v", t=4)
+        words = out_1.rearrange("z p v r -> p (z v r)").bitcast(I32)
+        for h in range(2):
+            nc.vector.tensor_tensor(s[h][:], near_m[h][:], far[h][:], ALU.subtract)
+        for h in range(2):
+            nc.scalar.activation(y[h][:], s[h][:], ACT.Relu)
+            nc.sync.dma_start(out_rows[:, :, H * h : H * (h + 1)], y[h][:])
+        for h in range(2):
+            nc.vector.tensor_scalar_max(yb[h][:], s[h][:].rearrange("p t v -> p v t"), 0.0)
+        for h in range(2):
+            quantize(yc[h][:], ys[:, H * h : H * (h + 1)], yb[h][:].rearrange("p v t -> p (v t)"))
+            nc.sync.dma_start(words[:, H * h : H * (h + 1)], yc[h][:].bitcast(I32))
+        for q in range(4):
+            eng = nc.scalar if q % 2 else nc.sync
+            eng.dma_start(out_2[0, 4 * q : 4 * q + 4, :].bitcast(I32), ys[32 * q : 32 * q + 4, :].bitcast(I32))

@@ -26,119 +26,128 @@ def tile_picked_triplet_none_lo_kernel(tc, xT, w1, margin, offs, out_0, out_1, o
 
         offsets = sb.tile([P, 3 * V // 16], U16, name="offsets")
         x = [sb.tile([P, T], F32, name="x%d" % j) for j in range(4)]
-        w_raw = sb.tile([P, 4, N], F32, name="w_raw")
+        w_raw = [sb.tile([P, 4, N // 2], F32, name="w_raw%d" % c) for c in range(2)]
         mg = sb.tile([P, V], F32, name="mg")
         xv = xT.rearrange("(p j) t -> p j t", j=4)
+        wv = w1.rearrange("(p j) c -> p j c", j=4)
         nc.sync.dma_start(x[0][:], xv[:, 0, :])
         nc.sync.dma_start(offsets[:], offs)
-        nc.sync.dma_start(x[1][:], xv[:, 1, :])
-        nc.sync.dma_start(w_raw[:], w1.rearrange("(p j) c -> p j c", j=4))
-        nc.sync.dma_start(x[2][:], xv[:, 2, :])
-        nc.sync.dma_start(x[3][:], xv[:, 3, :])
+        for j in range(1, 4):
+            nc.sync.dma_start(x[j][:], xv[:, j, :])
+        for c in range(2):
+            nc.sync.dma_start(w_raw[c][:], wv[:, :, 256 * c : 256 * (c + 1)])
         nc.sync.dma_start(mg[:], margin)
 
+        a_rows = sb.tile([P, 4, V], BF16, name="a_rows", align_bytes=64)
         xb = [sb.tile([P, V, 4], BF16, name="xb%d" % r, align_bytes=64) for r in range(3)]
-        a_neg = sb.tile([P, H, 4], BF16, name="a_neg", align_bytes=64)
-        xc = [sb.tile([P, V], U32, name="xc%d" % r, align_bytes=64) for r in range(3)]
-        xs = [sb.tile([P, V], U8, name="xs%d" % r, align_bytes=64) for r in range(3)]
-        nc_codes = sb.tile([P, H], U32, name="nc_codes", align_bytes=64)
-        nc_scales = sb.tile([P, H], U8, name="nc_scales", align_bytes=64)
+        a_codes = sb.tile([P, V], U32, name="a_codes", align_bytes=64)
+        a_scales = sb.tile([P, V], U8, name="a_scales", align_bytes=64)
+        pn_codes = sb.tile([P, 2 * V], U32, name="pn_codes", align_bytes=64)
+        pn_scales = sb.tile([P, 2 * V], U8, name="pn_scales", align_bytes=64)
         wb = [sb.tile([P, 2, P, 4], BF16, name="wb%d" % u, align_bytes=64) for u in range(2)]
         wc = [sb.tile([P, 2 * P], U32, name="wc%d" % u, align_bytes=64) for u in range(2)]
         ws = [sb.tile([P, 2 * P], U8, name="ws%d" % u, align_bytes=64) for u in range(2)]
 
-        def gather(j, r):
-            nc.vector.tensor_copy(xb[r][:, :, j], x[j][:].indirect(offsets[:, 16 * r : 16 * (r + 1)]))
-
         def quantize(codes, scales, src):
             nc.vector.quantize_mx(out=codes.bitcast(FP8X4), scales=scales, in_=src)
 
-        for j in range(2):
-            for r in range(3):
-                gather(j, r)
+        for j in range(4):
+            nc.vector.tensor_copy(a_rows[:, j, :], x[j][:].indirect(offsets[:, 0:16]))
+            for r in (1, 2):
+                nc.vector.tensor_copy(xb[r][:, :, j], x[j][:].indirect(offsets[:, 16 * r : 16 * (r + 1)]))
 
-        w_view = w_raw[:].rearrange("p j (m t) -> p m j t", t=4)
-        nc.vector.tensor_copy(wb[0][:].rearrange("p t m j -> p m j t"), w_view[:, :, :, 0:2])
-        nc.scalar.copy(wb[1][:].rearrange("p t m j -> p m j t"), w_view[:, :, :, 2:4])
-        for u in range(2):
-            quantize(wc[u][:], ws[u][:], wb[u][:].rearrange("p t m j -> p (t m j)"))
+        nc.scalar.activation(
+            xb[0][:].rearrange("p (c i) j -> p c j i", i=4),
+            a_rows[:].rearrange("p j (c i) -> p c j i", i=4),
+            ACT.Copy,
+            scale=-1.0,
+        )
+        for r in (1, 2):
+            cols = slice(V * (r - 1), V * r)
+            quantize(pn_codes[:, cols], pn_scales[:, cols], xb[r][:].rearrange("p v j -> p (v j)"))
+        quantize(a_codes[:], a_scales[:], xb[0][:].rearrange("p v j -> p (v j)"))
 
-        for r in range(3):
-            gather(2, r)
+        def deal(copy, c, u):
+            copy(
+                wb[u][:, :, 64 * c : 64 * (c + 1), :].rearrange("p t m j -> p m j t"),
+                w_raw[c][:].rearrange("p j (m t) -> p m j t", t=4)[:, :, :, 2 * u : 2 * u + 2],
+            )
 
-        def passes(bank, terms):
-            for t in range(4):
-                cols = slice(P * (t % 2), P * (t % 2 + 1))
-                for i, (codes, scales) in enumerate(terms):
-                    nc.tensor.matmul_mx(
-                        out=bank[:, t, :],
-                        lhsT=wc[t // 2][:, cols].bitcast(FP8X4),
-                        lhsT_scale=ws[t // 2][:, cols],
-                        rhs=codes.bitcast(FP8X4),
-                        rhs_scale=scales,
-                        start=(i == 0),
-                        stop=(i == len(terms) - 1),
-                    )
+        deal(nc.scalar.copy, 0, 0)
+        deal(nc.scalar.copy, 0, 1)
+        deal(nc.vector.tensor_copy, 1, 0)
+        deal(nc.scalar.copy, 1, 1)
+        for t in range(2):
+            quantize(wc[0][:, P * t : P * (t + 1)], ws[0][:, P * t : P * (t + 1)], wb[0][:, t, :, :].rearrange("p m j -> p (m j)"))
+        quantize(wc[1][:], ws[1][:], wb[1][:].rearrange("p t m j -> p (t m j)"))
 
-        lo, hi = slice(0, H), slice(H, V)
-        bank_a = ps.tile([P, 4, H], F32, name="bank_a")
-        bank_p = ps.tile([P, 4, H], F32, name="bank_p")
-        bank_n = ps.tile([P, 4, H], F32, name="bank_n")
-        bank_d1 = ps.tile([P, 4, H], F32, name="bank_d1")
-        bank_d2 = ps.tile([P, 4, H], F32, name="bank_d2")
+        def product(out, t, terms):
+            cols = slice(P * (t % 2), P * (t % 2 + 1))
+            for i, (codes, scales) in enumerate(terms):
+                nc.tensor.matmul_mx(
+                    out=out,
+                    lhsT=wc[t // 2][:, cols].bitcast(FP8X4),
+                    lhsT_scale=ws[t // 2][:, cols],
+                    rhs=codes.bitcast(FP8X4),
+                    rhs_scale=scales,
+                    start=(i == 0),
+                    stop=(i == len(terms) - 1),
+                )
 
-        def f32(name):
-            return sb.tile([P, 4, H], F32, name=name)
+        neg_a = (a_codes[:], a_scales[:])
+        pos = (pn_codes[:, 0:V], pn_scales[:, 0:V])
+        neg = (pn_codes[:, V : 2 * V], pn_scales[:, V : 2 * V])
+        bank_a = ps.tile([P, V], F32, name="bank_a")
+        bank_pn = ps.tile([P, 2, V], F32, name="bank_pn")
+        d_near = [None] + [ps.tile([P, V], F32, name="d_near%d" % t) for t in range(1, 4)]
+        d_far = [None] + [ps.tile([P, V], F32, name="d_far%d" % t) for t in range(1, 4)]
 
-        a_hi, d1_hi, d2_hi = f32("a_hi"), f32("d1_hi"), f32("d2_hi")
-        near = [f32("near0"), f32("near1")]
-        far = [f32("far0"), f32("far1")]
-        near_m = [f32("near_m0"), f32("near_m1")]
-        s = [f32("s0"), f32("s1")]
-        y = [f32("y0"), f32("y1")]
+        product(bank_a[:], 0, [neg_a])
+        product(bank_pn[:].rearrange("p r v -> p (r v)"), 0, [(pn_codes[:], pn_scales[:])])
+        for t in range(1, 4):
+            product(d_near[t][:], t, [neg_a, pos])
+        for t in range(1, 4):
+            product(d_far[t][:], t, [neg_a, neg])
+
+        a0 = sb.tile([P, V], F32, name="a0")
+        d0 = sb.tile([P, 2, V], F32, name="d0")
+        nc.scalar.copy(a0[:], bank_a[:])
+        nc.vector.tensor_tensor(d0[:], bank_pn[:], a0[:].unsqueeze(1).to_broadcast([P, 2, V]), ALU.add)
+        d_near[0] = d0[:, 0, :]
+        d_far[0] = d0[:, 1, :]
+
+        near = [sb.tile([P, V], F32, name="near%d" % t) for t in range(4)]
+        far = [sb.tile([P, V], F32, name="far%d" % t) for t in range(4)]
+        near_m = [sb.tile([P, V], F32, name="near_m%d" % t) for t in range(4)]
+        s = sb.tile([P, 4, V], F32, name="s")
+        y = [sb.tile([P, 2, V], F32, name="y%d" % u) for u in range(2)]
         yb = [sb.tile([P, H, 4], BF16, name="yb%d" % h, align_bytes=64) for h in range(2)]
         yc = [sb.tile([P, H], U32, name="yc%d" % h, align_bytes=64) for h in range(2)]
         ys = sb.tile([P, V], U8, name="ys", align_bytes=64)
 
-        neg = (nc_codes[:], nc_scales[:])
-
-        gather(3, 0)
-        nc.scalar.activation(a_neg[:], xb[0][:, lo, :], ACT.Copy, scale=-1.0)
-        gather(3, 1)
-        quantize(xc[0][:, hi], xs[0][:, hi], xb[0][:, hi, :].rearrange("p v j -> p (v j)"))
-        quantize(xc[1][:], xs[1][:], xb[1][:].rearrange("p v j -> p (v j)"))
-        quantize(neg[0], neg[1], a_neg[:].rearrange("p v j -> p (v j)"))
-        passes(bank_a, [(xc[0][:, hi], xs[0][:, hi])])
-        passes(bank_p, [(xc[1][:, hi], xs[1][:, hi])])
-        passes(bank_d1, [neg, (xc[1][:, lo], xs[1][:, lo])])
-        gather(3, 2)
-        quantize(xc[2][:], xs[2][:], xb[2][:].rearrange("p v j -> p (v j)"))
-        passes(bank_n, [(xc[2][:, hi], xs[2][:, hi])])
-        passes(bank_d2, [neg, (xc[2][:, lo], xs[2][:, lo])])
-
-        def add_margin(h):
-            m = mg[:, H * h : H * (h + 1)].unsqueeze(1).to_broadcast([P, 4, H])
-            nc.vector.tensor_tensor(near_m[h][:], near[h][:], m, ALU.add)
-
-        nc.scalar.copy(a_hi[:], bank_a[:])
-        nc.scalar.activation(near[0][:], bank_d1[:], ACT.Square)
-        nc.vector.tensor_tensor(d1_hi[:], bank_p[:], a_hi[:], ALU.subtract)
-        nc.scalar.activation(near[1][:], d1_hi[:], ACT.Square)
-        add_margin(0)
-        nc.vector.tensor_tensor(d2_hi[:], bank_n[:], a_hi[:], ALU.subtract)
-        nc.scalar.activation(far[0][:], bank_d2[:], ACT.Square)
-        add_margin(1)
-        nc.scalar.activation(far[1][:], d2_hi[:], ACT.Square)
+        for t in (1, 0, 2, 3):
+            nc.scalar.activation(near[t][:], d_near[t][:], ACT.Square)
+        for t in range(4):
+            nc.scalar.activation(far[t][:], d_far[t][:], ACT.Square)
+        for t in (1, 0, 2, 3):
+            nc.vector.tensor_tensor(near_m[t][:], near[t][:], mg[:], ALU.add)
+        for t in range(3):
+            nc.vector.tensor_tensor(s[:, t, :], near_m[t][:], far[t][:], ALU.subtract)
+        for h in range(2):
+            cols = slice(H * h, H * (h + 1))
+            nc.vector.tensor_tensor(s[:, 3, cols], near_m[3][:, cols], far[3][:, cols], ALU.subtract)
 
         out_rows = out_0.rearrange("(p t) v -> p t v", t=4)
         words = out_1.rearrange("z p v r -> p (z v r)").bitcast(I32)
+        for u in range(2):
+            nc.scalar.activation(y[u][:], s[:, 2 * u : 2 * u + 2, :], ACT.Relu)
+            nc.sync.dma_start(out_rows[:, 2 * u : 2 * u + 2, :], y[u][:])
         for h in range(2):
-            nc.vector.tensor_tensor(s[h][:], near_m[h][:], far[h][:], ALU.subtract)
-        for h in range(2):
-            nc.scalar.activation(y[h][:], s[h][:], ACT.Relu)
-            nc.sync.dma_start(out_rows[:, :, H * h : H * (h + 1)], y[h][:])
-        for h in range(2):
-            nc.vector.tensor_scalar_max(yb[h][:], s[h][:].rearrange("p t v -> p v t"), 0.0)
+            nc.vector.tensor_scalar_max(
+                yb[h][:].rearrange("p (c i) t -> p c t i", i=4),
+                s[:, :, H * h : H * (h + 1)].rearrange("p t (c i) -> p c t i", i=4),
+                0.0,
+            )
         for h in range(2):
             quantize(yc[h][:], ys[:, H * h : H * (h + 1)], yb[h][:].rearrange("p v t -> p (v t)"))
             nc.sync.dma_start(words[:, H * h : H * (h + 1)], yc[h][:].bitcast(I32))

@@ -26,7 +26,7 @@ def tile_picked_triplet_none_lo_kernel(tc, xT, w1, margin, offs, out_0, out_1, o
 
         offsets = sb.tile([P, 3 * V // 16], U16, name="offsets")
         x = [sb.tile([P, T], F32, name="x%d" % j) for j in range(4)]
-        w_raw = [sb.tile([P, 4, N // 2], F32, name="w_raw%d" % c) for c in range(2)]
+        w_raw = sb.tile([P, 2, 4, N // 2], F32, name="w_raw")
         mg = sb.tile([P, V], F32, name="mg")
         xv = xT.rearrange("(p j) t -> p j t", j=4)
         wv = w1.rearrange("(p j) c -> p j c", j=4)
@@ -35,10 +35,11 @@ def tile_picked_triplet_none_lo_kernel(tc, xT, w1, margin, offs, out_0, out_1, o
         for j in range(1, 4):
             nc.sync.dma_start(x[j][:], xv[:, j, :])
         for c in range(2):
-            nc.sync.dma_start(w_raw[c][:], wv[:, :, 256 * c : 256 * (c + 1)])
+            nc.sync.dma_start(w_raw[:, c, :, :], wv[:, :, 256 * c : 256 * (c + 1)])
         nc.sync.dma_start(mg[:], margin)
 
-        a_rows = sb.tile([P, 4, V], BF16, name="a_rows", align_bytes=64)
+        rows01 = sb.tile([P, 2, 3 * V], BF16, name="rows01", align_bytes=64)
+        a_rows23 = sb.tile([P, 2, V], BF16, name="a_rows23", align_bytes=64)
         xb = [sb.tile([P, V, 4], BF16, name="xb%d" % r, align_bytes=64) for r in range(3)]
         a_codes = sb.tile([P, V], U32, name="a_codes", align_bytes=64)
         a_scales = sb.tile([P, V], U8, name="a_scales", align_bytes=64)
@@ -51,32 +52,26 @@ def tile_picked_triplet_none_lo_kernel(tc, xT, w1, margin, offs, out_0, out_1, o
         def quantize(codes, scales, src):
             nc.vector.quantize_mx(out=codes.bitcast(FP8X4), scales=scales, in_=src)
 
-        for j in range(4):
-            nc.vector.tensor_copy(a_rows[:, j, :], x[j][:].indirect(offsets[:, 0:16]))
+        for j in range(2):
+            nc.vector.tensor_copy(rows01[:, j, :], x[j][:].indirect(offsets[:]))
+        for r in (1, 2):
+            nc.scalar.copy(xb[r][:, :, 0:2], rows01[:, :, V * r : V * (r + 1)].rearrange("p j v -> p v j"))
+        nc.scalar.activation(xb[0][:, :, 0:2], rows01[:, :, 0:V].rearrange("p j v -> p v j"), ACT.Copy, scale=-1.0)
+        for j in (2, 3):
+            nc.vector.tensor_copy(a_rows23[:, j - 2, :], x[j][:].indirect(offsets[:, 0:16]))
             for r in (1, 2):
                 nc.vector.tensor_copy(xb[r][:, :, j], x[j][:].indirect(offsets[:, 16 * r : 16 * (r + 1)]))
+        nc.scalar.activation(xb[0][:, :, 2:4], a_rows23[:].rearrange("p j v -> p v j"), ACT.Copy, scale=-1.0)
 
-        nc.scalar.activation(
-            xb[0][:].rearrange("p (c i) j -> p c j i", i=4),
-            a_rows[:].rearrange("p j (c i) -> p c j i", i=4),
-            ACT.Copy,
-            scale=-1.0,
-        )
+        quantize(a_codes[:], a_scales[:], xb[0][:].rearrange("p v j -> p (v j)"))
         for r in (1, 2):
             cols = slice(V * (r - 1), V * r)
             quantize(pn_codes[:, cols], pn_scales[:, cols], xb[r][:].rearrange("p v j -> p (v j)"))
-        quantize(a_codes[:], a_scales[:], xb[0][:].rearrange("p v j -> p (v j)"))
 
-        def deal(copy, c, u):
-            copy(
-                wb[u][:, :, 64 * c : 64 * (c + 1), :].rearrange("p t m j -> p m j t"),
-                w_raw[c][:].rearrange("p j (m t) -> p m j t", t=4)[:, :, :, 2 * u : 2 * u + 2],
-            )
-
-        deal(nc.scalar.copy, 0, 0)
-        deal(nc.scalar.copy, 0, 1)
-        deal(nc.vector.tensor_copy, 1, 0)
-        deal(nc.scalar.copy, 1, 1)
+        w_cols = w_raw[:].rearrange("p c j (m t) -> p c m j t", t=4)
+        for c in range(2):
+            nc.scalar.copy(wb[0][:, :, 64 * c : 64 * (c + 1), :].rearrange("p t m j -> p m j t"), w_cols[:, c, :, :, 0:2])
+        nc.scalar.copy(wb[1][:].rearrange("p t (c m) j -> p c m j t", c=2), w_cols[:, :, :, :, 2:4])
         for t in range(2):
             quantize(wc[0][:, P * t : P * (t + 1)], ws[0][:, P * t : P * (t + 1)], wb[0][:, t, :, :].rearrange("p m j -> p (m j)"))
         quantize(wc[1][:], ws[1][:], wb[1][:].rearrange("p t m j -> p (t m j)"))
@@ -97,24 +92,25 @@ def tile_picked_triplet_none_lo_kernel(tc, xT, w1, margin, offs, out_0, out_1, o
         neg_a = (a_codes[:], a_scales[:])
         pos = (pn_codes[:, 0:V], pn_scales[:, 0:V])
         neg = (pn_codes[:, V : 2 * V], pn_scales[:, V : 2 * V])
-        bank_a = ps.tile([P, V], F32, name="bank_a")
-        bank_pn = ps.tile([P, 2, V], F32, name="bank_pn")
+        bank_an = ps.tile([P, 2, V], F32, name="bank_an")
+        bank_p = ps.tile([P, V], F32, name="bank_p")
         d_near = [None] + [ps.tile([P, V], F32, name="d_near%d" % t) for t in range(1, 4)]
         d_far = [None] + [ps.tile([P, V], F32, name="d_far%d" % t) for t in range(1, 4)]
+        a0 = sb.tile([P, V], F32, name="a0")
+        d_near[0] = sb.tile([P, V], F32, name="d_near0")
+        d_far[0] = sb.tile([P, V], F32, name="d_far0")
 
-        product(bank_a[:], 0, [neg_a])
-        product(bank_pn[:].rearrange("p r v -> p (r v)"), 0, [(pn_codes[:], pn_scales[:])])
-        for t in range(1, 4):
+        product(bank_an[:, 0, :], 0, [neg_a])
+        product(bank_p[:], 0, [pos])
+        nc.vector.tensor_copy(a0[:], bank_an[:, 0, :])
+        nc.vector.tensor_tensor(d_near[0][:], bank_p[:], a0[:], ALU.add)
+        product(d_near[1][:], 1, [neg_a, pos])
+        product(bank_an[:, 1, :], 0, [neg])
+        nc.vector.tensor_tensor(d_far[0][:], bank_an[:, 1, :], a0[:], ALU.add)
+        for t in (2, 3):
             product(d_near[t][:], t, [neg_a, pos])
         for t in range(1, 4):
             product(d_far[t][:], t, [neg_a, neg])
-
-        a0 = sb.tile([P, V], F32, name="a0")
-        d0 = sb.tile([P, 2, V], F32, name="d0")
-        nc.scalar.copy(a0[:], bank_a[:])
-        nc.vector.tensor_tensor(d0[:], bank_pn[:], a0[:].unsqueeze(1).to_broadcast([P, 2, V]), ALU.add)
-        d_near[0] = d0[:, 0, :]
-        d_far[0] = d0[:, 1, :]
 
         near = [sb.tile([P, V], F32, name="near%d" % t) for t in range(4)]
         far = [sb.tile([P, V], F32, name="far%d" % t) for t in range(4)]

@@ -14,7 +14,9 @@ ACT = mybir.ActivationFunctionType
 
 P = 128
 K, T, V, N = 512, 2048, 256, 512
-H = V // 2
+WORD = 4
+HALF = V // 2
+THIRD = V // 16
 FLOPS = 2 * K * N * 3 * V
 
 
@@ -24,129 +26,139 @@ def tile_picked_triplet_none_lo_kernel(tc, xT, w1, margin, offs, out_0, out_1, o
         sb = ctx.enter_context(tc.tile_pool(name="sb", bufs=1))
         ps = ctx.enter_context(tc.psum_pool(name="ps", bufs=1))
 
-        offsets = sb.tile([P, 3 * V // 16], U16, name="offsets")
-        x = [sb.tile([P, T], F32, name="x%d" % j) for j in range(4)]
-        w_raw = sb.tile([P, 2, 4, N // 2], F32, name="w_raw")
-        mg = sb.tile([P, V], F32, name="mg")
-        xv = xT.rearrange("(p j) t -> p j t", j=4)
-        wv = w1.rearrange("(p j) c -> p j c", j=4)
-        nc.sync.dma_start(x[0][:], xv[:, 0, :])
+        def quantize(codes, scales, words):
+            nc.vector.quantize_mx(out=codes.bitcast(FP8X4), scales=scales, in_=words)
+
+        offsets = sb.tile([P, 3 * THIRD], U16, name="offsets")
+        x = [sb.tile([P, T], F32, name="x%d" % j) for j in range(WORD)]
+        w_raw = sb.tile([P, WORD, N], F32, name="w_raw")
+        margins = sb.tile([P, V], F32, name="margins")
+        x_rows = xT.rearrange("(p j) t -> p j t", j=WORD)
+        w_rows = w1.rearrange("(p j) c -> p j c", j=WORD)
+        nc.sync.dma_start(x[0][:], x_rows[:, 0, :])
         nc.sync.dma_start(offsets[:], offs)
-        for j in range(1, 4):
-            nc.sync.dma_start(x[j][:], xv[:, j, :])
-        for c in range(2):
-            nc.sync.dma_start(w_raw[:, c, :, :], wv[:, :, 256 * c : 256 * (c + 1)])
-        nc.sync.dma_start(mg[:], margin)
+        for j in range(1, WORD):
+            nc.sync.dma_start(x[j][:], x_rows[:, j, :])
+        for pair in (slice(0, 2), slice(2, 4)):
+            nc.sync.dma_start(w_raw[:, pair, :], w_rows[:, pair, :])
+        nc.sync.dma_start(margins[:], margin)
 
         rows01 = sb.tile([P, 2, 3 * V], BF16, name="rows01", align_bytes=64)
         a_rows23 = sb.tile([P, 2, V], BF16, name="a_rows23", align_bytes=64)
-        xb = [sb.tile([P, V, 4], BF16, name="xb%d" % r, align_bytes=64) for r in range(3)]
+        a_words = sb.tile([P, V, WORD], BF16, name="a_words", align_bytes=64)
+        pn_words = sb.tile([P, 2 * V, WORD], BF16, name="pn_words", align_bytes=64)
         a_codes = sb.tile([P, V], U32, name="a_codes", align_bytes=64)
         a_scales = sb.tile([P, V], U8, name="a_scales", align_bytes=64)
         pn_codes = sb.tile([P, 2 * V], U32, name="pn_codes", align_bytes=64)
         pn_scales = sb.tile([P, 2 * V], U8, name="pn_scales", align_bytes=64)
-        wb = [sb.tile([P, 2, P, 4], BF16, name="wb%d" % u, align_bytes=64) for u in range(2)]
-        wc = [sb.tile([P, 2 * P], U32, name="wc%d" % u, align_bytes=64) for u in range(2)]
-        ws = [sb.tile([P, 2 * P], U8, name="ws%d" % u, align_bytes=64) for u in range(2)]
-
-        def quantize(codes, scales, src):
-            nc.vector.quantize_mx(out=codes.bitcast(FP8X4), scales=scales, in_=src)
+        w_words = [sb.tile([P, 2, P, WORD], BF16, name="w_words%d" % u, align_bytes=64) for u in range(2)]
+        w_codes = [sb.tile([P, 2 * P], U32, name="w_codes%d" % u, align_bytes=64) for u in range(2)]
+        w_scales = [sb.tile([P, 2 * P], U8, name="w_scales%d" % u, align_bytes=64) for u in range(2)]
 
         for j in range(2):
             nc.vector.tensor_copy(rows01[:, j, :], x[j][:].indirect(offsets[:]))
-        for r in (1, 2):
-            nc.scalar.copy(xb[r][:, :, 0:2], rows01[:, :, V * r : V * (r + 1)].rearrange("p j v -> p v j"))
-        nc.scalar.activation(xb[0][:, :, 0:2], rows01[:, :, 0:V].rearrange("p j v -> p v j"), ACT.Copy, scale=-1.0)
+        nc.scalar.copy(pn_words[:, :, 0:2], rows01[:, :, V : 3 * V].rearrange("p j v -> p v j"))
+        nc.scalar.activation(a_words[:, :, 0:2], rows01[:, :, 0:V].rearrange("p j v -> p v j"), ACT.Copy, scale=-1.0)
+
         for j in (2, 3):
-            nc.vector.tensor_copy(a_rows23[:, j - 2, :], x[j][:].indirect(offsets[:, 0:16]))
-            for r in (1, 2):
-                nc.vector.tensor_copy(xb[r][:, :, j], x[j][:].indirect(offsets[:, 16 * r : 16 * (r + 1)]))
-        nc.scalar.activation(xb[0][:, :, 2:4], a_rows23[:].rearrange("p j v -> p v j"), ACT.Copy, scale=-1.0)
+            nc.vector.tensor_copy(a_rows23[:, j - 2, :], x[j][:].indirect(offsets[:, 0:THIRD]))
+            for r in range(2):
+                nc.vector.tensor_copy(
+                    pn_words[:, V * r : V * (r + 1), j],
+                    x[j][:].indirect(offsets[:, THIRD * (r + 1) : THIRD * (r + 2)]),
+                )
+        nc.scalar.activation(a_words[:, :, 2:4], a_rows23[:].rearrange("p j v -> p v j"), ACT.Copy, scale=-1.0)
 
-        quantize(a_codes[:], a_scales[:], xb[0][:].rearrange("p v j -> p (v j)"))
-        for r in (1, 2):
-            cols = slice(V * (r - 1), V * r)
-            quantize(pn_codes[:, cols], pn_scales[:, cols], xb[r][:].rearrange("p v j -> p (v j)"))
+        for r in range(2):
+            cols = slice(V * r, V * (r + 1))
+            quantize(pn_codes[:, cols], pn_scales[:, cols], pn_words[:, cols, :].rearrange("p v j -> p (v j)"))
+        quantize(a_codes[:], a_scales[:], a_words[:].rearrange("p v j -> p (v j)"))
 
-        w_cols = w_raw[:].rearrange("p c j (m t) -> p c m j t", t=4)
-        for c in range(2):
-            nc.scalar.copy(wb[0][:, :, 64 * c : 64 * (c + 1), :].rearrange("p t m j -> p m j t"), w_cols[:, c, :, :, 0:2])
-        nc.scalar.copy(wb[1][:].rearrange("p t (c m) j -> p c m j t", c=2), w_cols[:, :, :, :, 2:4])
+        w_cols = w_raw[:].rearrange("p j (m t) -> p m j t", t=WORD)
+        nc.scalar.copy(w_words[0][:, :, :, 0:2].rearrange("p t m j -> p m j t"), w_cols[:, :, 0:2, 0:2])
         for t in range(2):
-            quantize(wc[0][:, P * t : P * (t + 1)], ws[0][:, P * t : P * (t + 1)], wb[0][:, t, :, :].rearrange("p m j -> p (m j)"))
-        quantize(wc[1][:], ws[1][:], wb[1][:].rearrange("p t m j -> p (t m j)"))
+            nc.scalar.copy(w_words[0][:, t, :, 2:4], w_cols[:, :, 2:4, t])
+        nc.scalar.copy(w_words[1][:].rearrange("p t m j -> p m j t"), w_cols[:, :, :, 2:4])
+        for t in range(2):
+            cols = slice(P * t, P * (t + 1))
+            quantize(w_codes[0][:, cols], w_scales[0][:, cols], w_words[0][:, t, :, :].rearrange("p m j -> p (m j)"))
+        quantize(w_codes[1][:], w_scales[1][:], w_words[1][:].rearrange("p t m j -> p (t m j)"))
 
         def product(out, t, terms):
             cols = slice(P * (t % 2), P * (t % 2 + 1))
             for i, (codes, scales) in enumerate(terms):
                 nc.tensor.matmul_mx(
                     out=out,
-                    lhsT=wc[t // 2][:, cols].bitcast(FP8X4),
-                    lhsT_scale=ws[t // 2][:, cols],
+                    lhsT=w_codes[t // 2][:, cols].bitcast(FP8X4),
+                    lhsT_scale=w_scales[t // 2][:, cols],
                     rhs=codes.bitcast(FP8X4),
                     rhs_scale=scales,
                     start=(i == 0),
                     stop=(i == len(terms) - 1),
                 )
 
-        neg_a = (a_codes[:], a_scales[:])
-        pos = (pn_codes[:, 0:V], pn_scales[:, 0:V])
-        neg = (pn_codes[:, V : 2 * V], pn_scales[:, V : 2 * V])
+        minus_anchors = (a_codes[:], a_scales[:])
+        positives = (pn_codes[:, 0:V], pn_scales[:, 0:V])
+        negatives = (pn_codes[:, V : 2 * V], pn_scales[:, V : 2 * V])
+
         bank_an = ps.tile([P, 2, V], F32, name="bank_an")
         bank_p = ps.tile([P, V], F32, name="bank_p")
-        d_near = [None] + [ps.tile([P, V], F32, name="d_near%d" % t) for t in range(1, 4)]
-        d_far = [None] + [ps.tile([P, V], F32, name="d_far%d" % t) for t in range(1, 4)]
-        a0 = sb.tile([P, V], F32, name="a0")
-        d_near[0] = sb.tile([P, V], F32, name="d_near0")
-        d_far[0] = sb.tile([P, V], F32, name="d_far0")
+        d_near_psum = [ps.tile([P, V], F32, name="d_near%d" % t) for t in range(1, WORD)]
+        d_far_psum = [ps.tile([P, V], F32, name="d_far%d" % t) for t in range(1, WORD)]
+        minus_h_anchor0 = sb.tile([P, V], F32, name="minus_h_anchor0")
+        d_near = [sb.tile([P, V], F32, name="d_near0")] + d_near_psum
+        d_far = [sb.tile([P, V], F32, name="d_far0")] + d_far_psum
 
-        product(bank_an[:, 0, :], 0, [neg_a])
-        product(bank_p[:], 0, [pos])
-        nc.vector.tensor_copy(a0[:], bank_an[:, 0, :])
-        nc.vector.tensor_tensor(d_near[0][:], bank_p[:], a0[:], ALU.add)
-        product(d_near[1][:], 1, [neg_a, pos])
-        product(bank_an[:, 1, :], 0, [neg])
-        nc.vector.tensor_tensor(d_far[0][:], bank_an[:, 1, :], a0[:], ALU.add)
+        product(bank_an[:, 0, :], 0, [minus_anchors])
+        product(bank_p[:], 0, [positives])
+        nc.vector.tensor_copy(minus_h_anchor0[:], bank_an[:, 0, :])
+        nc.vector.tensor_tensor(d_near[0][:], bank_p[:], minus_h_anchor0[:], ALU.add)
+        product(d_near[1][:], 1, [minus_anchors, positives])
+        product(bank_an[:, 1, :], 0, [negatives])
+        nc.vector.tensor_tensor(d_far[0][:], bank_an[:, 1, :], minus_h_anchor0[:], ALU.add)
         for t in (2, 3):
-            product(d_near[t][:], t, [neg_a, pos])
-        for t in range(1, 4):
-            product(d_far[t][:], t, [neg_a, neg])
+            product(d_near[t][:], t, [minus_anchors, positives])
+        for t in range(1, WORD):
+            product(d_far[t][:], t, [minus_anchors, negatives])
 
-        near = [sb.tile([P, V], F32, name="near%d" % t) for t in range(4)]
-        far = [sb.tile([P, V], F32, name="far%d" % t) for t in range(4)]
-        near_m = [sb.tile([P, V], F32, name="near_m%d" % t) for t in range(4)]
-        s = sb.tile([P, 4, V], F32, name="s")
-        y = [sb.tile([P, 2, V], F32, name="y%d" % u) for u in range(2)]
-        yb = [sb.tile([P, H, 4], BF16, name="yb%d" % h, align_bytes=64) for h in range(2)]
-        yc = [sb.tile([P, H], U32, name="yc%d" % h, align_bytes=64) for h in range(2)]
-        ys = sb.tile([P, V], U8, name="ys", align_bytes=64)
+        near = [sb.tile([P, V], F32, name="near%d" % t) for t in range(WORD)]
+        far = [sb.tile([P, V], F32, name="far%d" % t) for t in range(WORD)]
+        near_margin = [sb.tile([P, V], F32, name="near_margin%d" % t) for t in range(WORD)]
+        loss = sb.tile([P, WORD, V], F32, name="loss")
+        y = sb.tile([P, WORD, V], F32, name="y")
+        y_words = [sb.tile([P, HALF, WORD], BF16, name="y_words%d" % h, align_bytes=64) for h in range(2)]
+        y_codes = sb.tile([P, V], U32, name="y_codes", align_bytes=64)
+        y_scales = sb.tile([P, V], U8, name="y_scales", align_bytes=64)
 
-        for t in (1, 0, 2, 3):
+        near_order = (1, 0, 2, 3)
+        for t in near_order:
             nc.scalar.activation(near[t][:], d_near[t][:], ACT.Square)
-        for t in range(4):
+        for t in range(WORD):
             nc.scalar.activation(far[t][:], d_far[t][:], ACT.Square)
-        for t in (1, 0, 2, 3):
-            nc.vector.tensor_tensor(near_m[t][:], near[t][:], mg[:], ALU.add)
+        for t in near_order:
+            nc.vector.tensor_tensor(near_margin[t][:], near[t][:], margins[:], ALU.add)
         for t in range(3):
-            nc.vector.tensor_tensor(s[:, t, :], near_m[t][:], far[t][:], ALU.subtract)
+            nc.vector.tensor_tensor(loss[:, t, :], near_margin[t][:], far[t][:], ALU.subtract)
         for h in range(2):
-            cols = slice(H * h, H * (h + 1))
-            nc.vector.tensor_tensor(s[:, 3, cols], near_m[3][:, cols], far[3][:, cols], ALU.subtract)
+            cols = slice(HALF * h, HALF * (h + 1))
+            nc.vector.tensor_tensor(loss[:, 3, cols], near_margin[3][:, cols], far[3][:, cols], ALU.subtract)
 
-        out_rows = out_0.rearrange("(p t) v -> p t v", t=4)
-        words = out_1.rearrange("z p v r -> p (z v r)").bitcast(I32)
-        for u in range(2):
-            nc.scalar.activation(y[u][:], s[:, 2 * u : 2 * u + 2, :], ACT.Relu)
-            nc.sync.dma_start(out_rows[:, 2 * u : 2 * u + 2, :], y[u][:])
+        out_rows = out_0.rearrange("(p t) v -> p t v", t=WORD)
+        out_words = out_1.rearrange("z p v r -> p (z v r)").bitcast(I32)
+        for groups in (slice(0, 2), slice(2, 3), slice(3, 4)):
+            nc.scalar.activation(y[:, groups, :], loss[:, groups, :], ACT.Relu)
+            nc.sync.dma_start(out_rows[:, groups, :], y[:, groups, :])
+
         for h in range(2):
             nc.vector.tensor_scalar_max(
-                yb[h][:].rearrange("p (c i) t -> p c t i", i=4),
-                s[:, :, H * h : H * (h + 1)].rearrange("p t (c i) -> p c t i", i=4),
+                y_words[h][:].rearrange("p (c i) t -> p c t i", i=4),
+                loss[:, :, HALF * h : HALF * (h + 1)].rearrange("p t (c i) -> p c t i", i=4),
                 0.0,
             )
         for h in range(2):
-            quantize(yc[h][:], ys[:, H * h : H * (h + 1)], yb[h][:].rearrange("p v t -> p (v t)"))
-            nc.sync.dma_start(words[:, H * h : H * (h + 1)], yc[h][:].bitcast(I32))
+            cols = slice(HALF * h, HALF * (h + 1))
+            quantize(y_codes[:, cols], y_scales[:, cols], y_words[h][:].rearrange("p v t -> p (v t)"))
+        nc.sync.dma_start(out_words, y_codes[:].bitcast(I32))
         for q in range(4):
-            eng = nc.scalar if q % 2 else nc.sync
-            eng.dma_start(out_2[0, 4 * q : 4 * q + 4, :].bitcast(I32), ys[32 * q : 32 * q + 4, :].bitcast(I32))
+            queue = nc.scalar if q % 2 else nc.sync
+            queue.dma_start(out_2[0, 4 * q : 4 * q + 4, :].bitcast(I32), y_scales[32 * q : 32 * q + 4, :].bitcast(I32))

from contextlib import ExitStack

import concourse.mybir as mybir

F32 = mybir.dt.float32
BF16 = mybir.dt.bfloat16
I32 = mybir.dt.int32
U32 = mybir.dt.uint32
U16 = mybir.dt.uint16
U8 = mybir.dt.uint8
FP8X4 = mybir.dt.float8_e4m3fn_x4
ALU = mybir.AluOpType
ACT = mybir.ActivationFunctionType

P = 128
K, T, V, N = 512, 2048, 256, 512
WORD = 4
HALF = V // 2
THIRD = V // 16
FLOPS = 2 * K * N * 3 * V


def tile_picked_triplet_none_lo_kernel(tc, xT, w1, margin, offs, out_0, out_1, out_2):
    nc = tc.nc
    with ExitStack() as ctx:
        sb = ctx.enter_context(tc.tile_pool(name="sb", bufs=1))
        ps = ctx.enter_context(tc.psum_pool(name="ps", bufs=1))

        def quantize(codes, scales, words):
            nc.vector.quantize_mx(out=codes.bitcast(FP8X4), scales=scales, in_=words)

        offsets = sb.tile([P, 3 * THIRD], U16, name="offsets")
        x = [sb.tile([P, T], F32, name="x%d" % j) for j in range(WORD)]
        w_raw = sb.tile([P, WORD, N], F32, name="w_raw")
        margins = sb.tile([P, V], F32, name="margins")
        x_rows = xT.rearrange("(p j) t -> p j t", j=WORD)
        w_rows = w1.rearrange("(p j) c -> p j c", j=WORD)
        nc.sync.dma_start(x[0][:], x_rows[:, 0, :])
        nc.sync.dma_start(offsets[:], offs)
        for j in range(1, WORD):
            nc.sync.dma_start(x[j][:], x_rows[:, j, :])
        for pair in (slice(0, 2), slice(2, 4)):
            nc.sync.dma_start(w_raw[:, pair, :], w_rows[:, pair, :])
        nc.sync.dma_start(margins[:], margin)

        rows01 = sb.tile([P, 2, 3 * V], BF16, name="rows01", align_bytes=64)
        a_rows23 = sb.tile([P, 2, V], BF16, name="a_rows23", align_bytes=64)
        a_words = sb.tile([P, V, WORD], BF16, name="a_words", align_bytes=64)
        pn_words = sb.tile([P, 2 * V, WORD], BF16, name="pn_words", align_bytes=64)
        a_codes = sb.tile([P, V], U32, name="a_codes", align_bytes=64)
        a_scales = sb.tile([P, V], U8, name="a_scales", align_bytes=64)
        pn_codes = sb.tile([P, 2 * V], U32, name="pn_codes", align_bytes=64)
        pn_scales = sb.tile([P, 2 * V], U8, name="pn_scales", align_bytes=64)
        w_words = [sb.tile([P, 2, P, WORD], BF16, name="w_words%d" % u, align_bytes=64) for u in range(2)]
        w_codes = [sb.tile([P, 2 * P], U32, name="w_codes%d" % u, align_bytes=64) for u in range(2)]
        w_scales = [sb.tile([P, 2 * P], U8, name="w_scales%d" % u, align_bytes=64) for u in range(2)]

        for j in range(2):
            nc.vector.tensor_copy(rows01[:, j, :], x[j][:].indirect(offsets[:]))
        nc.scalar.copy(pn_words[:, :, 0:2], rows01[:, :, V : 3 * V].rearrange("p j v -> p v j"))
        nc.scalar.activation(a_words[:, :, 0:2], rows01[:, :, 0:V].rearrange("p j v -> p v j"), ACT.Copy, scale=-1.0)

        for j in (2, 3):
            nc.vector.tensor_copy(a_rows23[:, j - 2, :], x[j][:].indirect(offsets[:, 0:THIRD]))
            for r in range(2):
                nc.vector.tensor_copy(
                    pn_words[:, V * r : V * (r + 1), j],
                    x[j][:].indirect(offsets[:, THIRD * (r + 1) : THIRD * (r + 2)]),
                )
        nc.scalar.activation(a_words[:, :, 2:4], a_rows23[:].rearrange("p j v -> p v j"), ACT.Copy, scale=-1.0)

        for r in range(2):
            cols = slice(V * r, V * (r + 1))
            quantize(pn_codes[:, cols], pn_scales[:, cols], pn_words[:, cols, :].rearrange("p v j -> p (v j)"))
        quantize(a_codes[:], a_scales[:], a_words[:].rearrange("p v j -> p (v j)"))

        w_cols = w_raw[:].rearrange("p j (m t) -> p m j t", t=WORD)
        nc.scalar.copy(w_words[0][:, :, :, 0:2].rearrange("p t m j -> p m j t"), w_cols[:, :, 0:2, 0:2])
        for t in range(2):
            nc.scalar.copy(w_words[0][:, t, :, 2:4], w_cols[:, :, 2:4, t])
        nc.scalar.copy(w_words[1][:].rearrange("p t m j -> p m j t"), w_cols[:, :, :, 2:4])
        for t in range(2):
            cols = slice(P * t, P * (t + 1))
            quantize(w_codes[0][:, cols], w_scales[0][:, cols], w_words[0][:, t, :, :].rearrange("p m j -> p (m j)"))
        quantize(w_codes[1][:], w_scales[1][:], w_words[1][:].rearrange("p t m j -> p (t m j)"))

        def product(out, t, terms):
            cols = slice(P * (t % 2), P * (t % 2 + 1))
            for i, (codes, scales) in enumerate(terms):
                nc.tensor.matmul_mx(
                    out=out,
                    lhsT=w_codes[t // 2][:, cols].bitcast(FP8X4),
                    lhsT_scale=w_scales[t // 2][:, cols],
                    rhs=codes.bitcast(FP8X4),
                    rhs_scale=scales,
                    start=(i == 0),
                    stop=(i == len(terms) - 1),
                )

        minus_anchors = (a_codes[:], a_scales[:])
        positives = (pn_codes[:, 0:V], pn_scales[:, 0:V])
        negatives = (pn_codes[:, V : 2 * V], pn_scales[:, V : 2 * V])

        bank_an = ps.tile([P, 2, V], F32, name="bank_an")
        bank_p = ps.tile([P, V], F32, name="bank_p")
        d_near_psum = [ps.tile([P, V], F32, name="d_near%d" % t) for t in range(1, WORD)]
        d_far_psum = [ps.tile([P, V], F32, name="d_far%d" % t) for t in range(1, WORD)]
        minus_h_anchor0 = sb.tile([P, V], F32, name="minus_h_anchor0")
        d_near = [sb.tile([P, V], F32, name="d_near0")] + d_near_psum
        d_far = [sb.tile([P, V], F32, name="d_far0")] + d_far_psum

        product(bank_an[:, 0, :], 0, [minus_anchors])
        product(bank_p[:], 0, [positives])
        nc.vector.tensor_copy(minus_h_anchor0[:], bank_an[:, 0, :])
        nc.vector.tensor_tensor(d_near[0][:], bank_p[:], minus_h_anchor0[:], ALU.add)
        product(d_near[1][:], 1, [minus_anchors, positives])
        product(bank_an[:, 1, :], 0, [negatives])
        nc.vector.tensor_tensor(d_far[0][:], bank_an[:, 1, :], minus_h_anchor0[:], ALU.add)
        for t in (2, 3):
            product(d_near[t][:], t, [minus_anchors, positives])
        for t in range(1, WORD):
            product(d_far[t][:], t, [minus_anchors, negatives])

        near = [sb.tile([P, V], F32, name="near%d" % t) for t in range(WORD)]
        far = [sb.tile([P, V], F32, name="far%d" % t) for t in range(WORD)]
        near_margin = [sb.tile([P, V], F32, name="near_margin%d" % t) for t in range(WORD)]
        loss = sb.tile([P, WORD, V], F32, name="loss")
        y = sb.tile([P, WORD, V], F32, name="y")
        y_words = [sb.tile([P, HALF, WORD], BF16, name="y_words%d" % h, align_bytes=64) for h in range(2)]
        y_codes = sb.tile([P, V], U32, name="y_codes", align_bytes=64)
        y_scales = sb.tile([P, V], U8, name="y_scales", align_bytes=64)

        near_order = (1, 0, 2, 3)
        for t in near_order:
            nc.scalar.activation(near[t][:], d_near[t][:], ACT.Square)
        for t in range(WORD):
            nc.scalar.activation(far[t][:], d_far[t][:], ACT.Square)
        for t in near_order:
            nc.vector.tensor_tensor(near_margin[t][:], near[t][:], margins[:], ALU.add)
        for t in range(3):
            nc.vector.tensor_tensor(loss[:, t, :], near_margin[t][:], far[t][:], ALU.subtract)
        for h in range(2):
            cols = slice(HALF * h, HALF * (h + 1))
            nc.vector.tensor_tensor(loss[:, 3, cols], near_margin[3][:, cols], far[3][:, cols], ALU.subtract)

        out_rows = out_0.rearrange("(p t) v -> p t v", t=WORD)
        out_words = out_1.rearrange("z p v r -> p (z v r)").bitcast(I32)
        for groups in (slice(0, 2), slice(2, 3), slice(3, 4)):
            nc.scalar.activation(y[:, groups, :], loss[:, groups, :], ACT.Relu)
            nc.sync.dma_start(out_rows[:, groups, :], y[:, groups, :])

        for h in range(2):
            nc.vector.tensor_scalar_max(
                y_words[h][:].rearrange("p (c i) t -> p c t i", i=4),
                loss[:, :, HALF * h : HALF * (h + 1)].rearrange("p t (c i) -> p c t i", i=4),
                0.0,
            )
        for h in range(2):
            cols = slice(HALF * h, HALF * (h + 1))
            quantize(y_codes[:, cols], y_scales[:, cols], y_words[h][:].rearrange("p v t -> p (v t)"))
        nc.sync.dma_start(out_words, y_codes[:].bitcast(I32))
        for q in range(4):
            queue = nc.scalar if q % 2 else nc.sync
            queue.dma_start(out_2[0, 4 * q : 4 * q + 4, :].bitcast(I32), y_scales[32 * q : 32 * q + 4, :].bitcast(I32))
